import numpy as np
import ml_dtypes


def mxq(x, axis, fmt="e4m3"):
    dtype, down = {"e4m3": (ml_dtypes.float8_e4m3fn, 7), "e5m2": (ml_dtypes.float8_e5m2, 14)}[fmt]
    v = np.moveaxis(np.asarray(x, np.float32).astype(ml_dtypes.bfloat16).astype(np.float64), axis, -1)
    blocks = v.reshape(v.shape[:-1] + (-1, 32))
    amax = np.abs(blocks).max(-1, keepdims=True)
    byte = np.maximum(np.where(amax > 0, np.frexp(amax)[1] - 1 + 127, 0) - down, 1)
    scale = np.exp2(byte - 127.0)
    codes = (blocks / scale).astype(np.float32).astype(dtype).astype(np.float64)
    return np.moveaxis((codes * scale).reshape(v.shape), -1, axis)


WIDE = False


def mx_kscale(k):
    if not WIDE:
        return np.ones(k)
    levels = np.array([10, -10, 5, -5, 0])
    if k % 512:
        return np.exp2(np.random.permutation(np.resize(levels, k // 32))).repeat(32)
    a = np.empty((k // 512, 16))
    for p in range(k // 512):
        a[p, :8] = np.random.permutation(np.resize(levels, 8))
        for g in range(8):
            far = levels[np.abs(levels - a[p, g]) >= 10]
            a[p, g + 8] = far[np.random.randint(len(far))]
    return np.exp2(a.ravel()).repeat(32)


BF16 = ml_dtypes.bfloat16


def bf(x):
    return np.asarray(x, np.float32).astype(BF16)


def f64(x):
    return np.asarray(x).astype(np.float64)


N, D, H = 1536, 512, 512


def sigmoid(z):
    return 0.5 * (1.0 + np.tanh(0.5 * z))


def setup_inputs():
    s, v, u = mx_kscale(D), mx_kscale(H), mx_kscale(N)
    return {"x": bf(np.random.standard_normal((N, D)) * s),
            "r": bf(np.random.standard_normal((N, H)) * v),
            "c": bf(np.random.standard_normal((N, H))),
            "wx": bf(np.random.standard_normal((D, 4 * H)) / np.sqrt(D) / s[:, None]),
            "wr": bf(np.random.standard_normal((H, 4 * H)) / np.sqrt(H) / v[:, None]),
            "b": bf(0.4 * np.random.standard_normal(4 * H)),
            "peep": bf(0.4 * np.random.standard_normal((3, H))),
            "d": bf((1.0 + 0.1 * np.random.standard_normal(N)) * u),
            "a": bf(2.0 * np.random.standard_normal((N, N)) / np.sqrt(N) / u)}


def reference(x, r, c, wx, wr, b, peep, d, a):
    c_old, p = f64(c), f64(peep)
    zx = mxq(f64(x), 1, "e4m3") @ mxq(f64(wx), 0, "e4m3")
    zr = mxq(f64(r), 1, "e4m3") @ mxq(f64(wr), 0, "e4m3")
    z = zx + zr + f64(b)
    gate_i = sigmoid(z[:, :H] + p[0] * c_old)
    gate_f = sigmoid(z[:, H:2 * H] + p[1] * c_old)
    cand = np.tanh(z[:, 2 * H:3 * H])
    c_new = gate_f * c_old + gate_i * cand
    gate_o = sigmoid(z[:, 3 * H:] + p[2] * c_new)
    m = gate_o * np.tanh(c_new) * f64(d)[:, None]
    r_new = mxq(f64(a), 1, "e4m3") @ mxq(m, 0, "e4m3")
    return r_new, c_new

from contextlib import ExitStack

import concourse.mybir as mybir
from concourse.masks import make_identity

N, D, H = 1536, 512, 512
FLOPS = 2 * N * (D + H) * 4 * H + 2 * N * N * H

F32 = mybir.dt.float32
BF16 = mybir.dt.bfloat16
U32 = mybir.dt.uint32
U8 = mybir.dt.uint8
FP8X4 = mybir.dt.float8_e4m3fn_x4
ACT = mybir.ActivationFunctionType
ALU = mybir.AluOpType

P = 128
PACK = 4
GROUP = 512
NG = N // GROUP
NHB = H // P


def tile_node_mixing_peephole_lstm_f4_kernel(tc, x, r, c, wx, wr, b, peep, d, a, r_new, c_new):
    nc = tc.nc
    with ExitStack() as ctx:
        const = ctx.enter_context(tc.tile_pool(name="const", bufs=1))
        raw = ctx.enter_context(tc.tile_pool(name="raw", bufs=1))
        grp = ctx.enter_context(tc.tile_pool(name="grp", bufs=2))
        codes = ctx.enter_context(tc.tile_pool(name="codes", bufs=1))
        work = ctx.enter_context(tc.tile_pool(name="work", bufs=2))
        zps = ctx.enter_context(tc.psum_pool(name="zps", bufs=4))
        tps = ctx.enter_context(tc.psum_pool(name="tps", bufs=4))
        ctx.enter_context(tc.manual_schedule())

        warm = const.tile([P, 1], F32, name="warm")
        nc.vector.memset(warm[:], 0.0)
        nc.scalar.activation(out=warm[:], in_=warm[:], func=ACT.Sigmoid)
        vec_rows = const.tile([P, P], BF16, name="vec_rows")
        nc.vector.memset(vec_rows[:], 0.0)
        ident = const.tile([P, P], F32, name="ident")
        make_identity(nc, ident[:])
        ident_bf = const.tile([P, P], BF16, name="ident_bf")
        make_identity(nc, ident_bf[:])

        def load_rows(src, g, label, parts):
            t = raw.tile([P, PACK, 512], BF16, name=f"{label}{g}")
            view = src[g * GROUP:(g + 1) * GROUP, :].rearrange("(p t) k -> p t k", t=PACK)
            step = PACK // parts
            for i in range(parts):
                nc.sync.dma_start(out=t[:, i * step:(i + 1) * step, :], in_=view[:, i * step:(i + 1) * step, :])
            return t

        w_raw = {}

        def load_w(m, half, gate):
            src = wx if m == "wx" else wr
            t = raw.tile([P, PACK, 256], BF16, name="w_raw", tag=f"{m}_{gate}")
            c0 = gate * 512 + half * 256
            nc.sync.dma_start(out=t[:], in_=src[:, c0:c0 + 256].rearrange("(p j) w -> p j w", j=PACK))
            w_raw[m, half, gate] = t

        a_raw = {}

        def load_a(j):
            t = raw.tile([P, N], BF16, name=f"a_raw{j}", tag="a_raw", bufs=6)
            nc.sync.dma_start(out=t[:], in_=a[j * P:(j + 1) * P, :])
            a_raw[j] = t

        x_raw, r_raw, c_raw = {}, {}, {}
        nc.scalar.dma_start(out=vec_rows[0:16, :], in_=b.rearrange("(q w) -> q w", w=P))
        nc.scalar.dma_start(out=vec_rows[16:28, :], in_=peep.rearrange("k (q w) -> (k q) w", w=P))
        d_sb = const.tile([P, NG, PACK], BF16, name="d_sb")
        nc.scalar.dma_start(out=d_sb[:], in_=d.rearrange("(g p t) -> p g t", p=P, t=PACK))
        load_w("wx", 0, 0)
        x_raw[0] = load_rows(x, 0, "x", 2)
        load_w("wr", 0, 0)
        r_raw[0] = load_rows(r, 0, "r", 2)
        load_w("wx", 0, 1)
        load_w("wr", 0, 1)
        c_raw[0] = load_rows(c, 0, "c", 1)
        for gate in (2, 3):
            load_w("wx", 0, gate)
            load_w("wr", 0, gate)
        for g in (1, 2):
            x_raw[g] = load_rows(x, g, "x", 1)
            r_raw[g] = load_rows(r, g, "r", 1)
            c_raw[g] = load_rows(c, g, "c", 1)
        load_a(0)
        load_a(1)

        xq, xs, rq, rs = {}, {}, {}, {}
        for g in range(NG):
            xq[g] = codes.tile([P, GROUP], U32, name=f"xq{g}", align_bytes=256)
            xs[g] = codes.tile([P, GROUP], U8, name=f"xs{g}", align_bytes=256)
            rq[g] = codes.tile([P, GROUP], U32, name=f"rq{g}", align_bytes=256)
            rs[g] = codes.tile([P, GROUP], U8, name=f"rs{g}", align_bytes=256)
        wq, ws = {}, {}
        for m in ("wx", "wr"):
            for half in range(2):
                wq[m, half] = codes.tile([P, 1024], U32, name=f"{m}q{half}", align_bytes=256)
                ws[m, half] = codes.tile([P, 1024], U8, name=f"{m}s{half}", align_bytes=256)
        aq = codes.tile([P, NG, N], U32, name="aq", align_bytes=256)
        a_s = codes.tile([P, NG, N], U8, name="a_s", align_bytes=256)
        mq = codes.tile([P, NG, H], U32, name="mq", align_bytes=256)
        ms = codes.tile([P, NG, H], U8, name="ms", align_bytes=256)
        cT = {}
        for g in range(NG):
            for hb in range(NHB):
                cT[g, hb] = codes.tile([P, GROUP], BF16, name=f"cT{g}_{hb}")
        vec = const.tile([P, 28], F32, name="vec")

        def bias_col(gate, hb):
            i = gate * 4 + hb
            return vec[:, i:i + 1]

        def peep_col(k, hb):
            i = 16 + k * 4 + hb
            return vec[:, i:i + 1]

        copy = {"S": nc.scalar.copy, "V": nc.vector.tensor_copy, "G": nc.gpsimd.tensor_copy}

        pending = []

        def flush(n=99):
            while pending and n > 0:
                pending.pop(0)()
                n -= 1

        def xr_piece(src, q, s, half, eng):
            bank = tps.tile([P, 2, 2, P], F32, name="bank", tag="tr")
            for i in range(2):
                words = src[:, 2 * half + i, :].bitcast(F32)
                for u in range(2):
                    nc.tensor.transpose(bank[:, i, u, :], words[:, u:256:2], ident[:])
            g4 = grp.tile([P, 256, PACK], BF16, name="g4", tag="g4", bufs=6, align_bytes=256)
            copy[eng](
                out=g4[:].rearrange("p n k -> p (n k)").bitcast(F32).rearrange("p (i n u) -> p i n u", i=2, u=2),
                in_=bank[:].rearrange("p i u n -> p i n u"),
            )
            cols = slice(half * 256, (half + 1) * 256)

            def quant():
                nc.vector.quantize_mx(out=q[:, cols].bitcast(FP8X4), scales=s[:, cols], in_=g4[:].rearrange("p n k -> p (n k)"))

            pending.append(quant)

        def a_piece(pair, q, eng):
            bank = tps.tile([P, 2, 2, P], F32, name="bank", tag="tr")
            for i in range(2):
                words = a_raw[2 * pair + i][:].bitcast(F32)
                for u in range(2):
                    nc.tensor.transpose(bank[:, i, u, :], words[:, 256 * q + u:256 * (q + 1):2], ident[:])
            g4 = grp.tile([P, 256, PACK], BF16, name="g4", tag="g4", bufs=6, align_bytes=256)
            copy[eng](
                out=g4[:].rearrange("p n k -> p (n k)").bitcast(F32).rearrange("p (i n u) -> p i n u", i=2, u=2),
                in_=bank[:].rearrange("p i u n -> p i n u"),
            )
            cols = slice(pair * 256, (pair + 1) * 256)

            def quant():
                nc.vector.quantize_mx(out=aq[:, q, cols].bitcast(FP8X4), scales=a_s[:, q, cols], in_=g4[:].rearrange("p n k -> p (n k)"))

            pending.append(quant)

        def c_piece(g, hb, eng):
            bank = tps.tile([P, PACK, P], BF16, name="cbank", tag="tr")
            for t in range(PACK):
                nc.tensor.transpose(bank[:, t, :], c_raw[g][:, t, hb * P:(hb + 1) * P], ident_bf[:])
            copy[eng](out=cT[g, hb][:], in_=bank[:].rearrange("p t n -> p (t n)"))

        def w_piece(m, half, gate, eng):
            wg = grp.tile([P, 256, PACK], BF16, name="wg", tag="wg", bufs=6, align_bytes=256)
            copy[eng](
                out=wg[:].rearrange("p (n i) k -> p n k i", i=4),
                in_=w_raw[m, half, gate][:].rearrange("p k (n i) -> p n k i", i=4),
            )
            cols = slice(gate * 256, (gate + 1) * 256)

            def quant():
                nc.vector.quantize_mx(
                    out=wq[m, half][:, cols].bitcast(FP8X4),
                    scales=ws[m, half][:, cols],
                    in_=wg[:].rearrange("p n k -> p (n k)"),
                )

            pending.append(quant)

        units = [(0, 0), (1, 0), (0, 1), (1, 1), (0, 2), (1, 2), (2, 0), (2, 1), (2, 2), (3, 0), (3, 1), (3, 2)]
        z = {}

        def z_mm(s, gate):
            hb, g = units[s]
            acc = zps.tile([P, GROUP], F32, name="acc", tag="z")
            c0 = gate * 256 + (hb % 2) * P
            half = hb // 2
            for i, (m, q, sc) in enumerate((("wx", xq, xs), ("wr", rq, rs))):
                nc.tensor.matmul_mx(
                    out=acc[:],
                    lhsT=wq[m, half][:, c0:c0 + P].bitcast(FP8X4),
                    lhsT_scale=ws[m, half][:, c0:c0 + P],
                    rhs=q[g][:].bitcast(FP8X4),
                    rhs_scale=sc[g][:],
                    start=(i == 0),
                    stop=(i == 1),
                )
            z[s, gate] = acc

        state = {}
        cst = {}

        def m_mul(s):
            st = state[s]
            m = work.tile([P, GROUP], F32, name="m", tag="m")
            nc.vector.tensor_mul(out=m[:], in0=st["o"][:], in1=st["th"][:])
            st["m"] = m

        def m_transpose(s):
            st = state[s]
            m = st["m"]
            bank = tps.tile([P, PACK, P], F32, name="mbank", tag="tr")
            for t in range(PACK):
                nc.tensor.transpose(bank[:, t, :], m[:, t * P:(t + 1) * P], ident[:])
            st["mbank"] = bank

        def cn_out(s):
            hb, g = units[s]
            cn = state[s]["cn"]
            cbank = tps.tile([P, PACK, P], F32, name="cnbank", tag="tr")
            for t in range(PACK):
                nc.tensor.transpose(cbank[:, t, :], cn[:, t * P:(t + 1) * P], ident[:])
            half = hb // 2
            if (g, half) not in cst:
                cst[g, half] = work.tile([P, PACK, 256], F32, name=f"cst{g}{half}", tag="cst", bufs=3)
            ct = cst[g, half]
            nc.scalar.copy(out=ct[:, :, (hb % 2) * P:(hb % 2 + 1) * P], in_=cbank[:])
            if hb % 2 == 1:
                view = c_new.rearrange("(g p t) h -> g p t h", p=P, t=PACK)[g]
                nc.sync.dma_start(out=view[:, :, half * 256:(half + 1) * 256], in_=ct[:])

        def m_evac(s):
            hb, g = units[s]
            st = state[s]
            mg = grp.tile([P, P, PACK], BF16, name="mg", tag="mg", bufs=3, align_bytes=256)
            nc.vector.tensor_mul(
                out=mg[:],
                in0=st["mbank"][:].rearrange("p t h -> p h t"),
                in1=d_sb[:, g, :].unsqueeze(1).to_broadcast([P, P, PACK]),
            )
            cols = slice(hb * P, (hb + 1) * P)

            def quant():
                nc.vector.quantize_mx(out=mq[:, g, cols].bitcast(FP8X4), scales=ms[:, g, cols], in_=mg[:].rearrange("p h t -> p (h t)"))

            return quant

        out_r = r_new.rearrange("(a p) h -> p a h", p=P)

        def mix_piece(j0, h0, w, eng, pool=None):
            nj = 512 // w
            bank = tps.tile([P, nj, w], F32, name="rbank", tag="tr")
            for i in range(nj):
                j = j0 + i
                for g in range(NG):
                    nc.tensor.matmul_mx(
                        out=bank[:, i, :],
                        lhsT=aq[:, g, j * P:(j + 1) * P].bitcast(FP8X4),
                        lhsT_scale=a_s[:, g, j * P:(j + 1) * P],
                        rhs=mq[:, g, h0:h0 + w].bitcast(FP8X4),
                        rhs_scale=ms[:, g, h0:h0 + w],
                        start=(g == 0),
                        stop=(g == NG - 1),
                    )
            rst = work.tile([P, nj, w], F32, name="rst", tag="rst", bufs=6)
            copy[eng](out=rst[:], in_=bank[:])
            nc.sync.dma_start(out=out_r[:, j0:j0 + nj, h0:h0 + w], in_=rst[:])

        w_piece("wx", 0, 0, "V")
        xr_piece(x_raw[0], xq[0], xs[0], 0, "S")
        xr_piece(x_raw[0], xq[0], xs[0], 1, "S")
        w_piece("wr", 0, 0, "V")
        flush()
        xr_piece(r_raw[0], rq[0], rs[0], 0, "S")
        xr_piece(r_raw[0], rq[0], rs[0], 1, "V")
        w_piece("wx", 0, 1, "V")
        vbank = tps.tile([P, P], BF16, name="vbank", tag="tr")
        nc.tensor.transpose(vbank[:], vec_rows[:], ident_bf[:])
        nc.vector.tensor_copy(out=vec[:], in_=vbank[:, 0:28])
        w_piece("wr", 0, 1, "S")
        flush()
        c_piece(0, 0, "S")
        c_piece(0, 1, "S")
        z_mm(0, 0)
        z_mm(0, 1)
        w_piece("wx", 0, 2, "V")
        w_piece("wr", 0, 2, "V")
        flush()
        z_mm(0, 2)
        w_piece("wx", 0, 3, "V")
        w_piece("wr", 0, 3, "S")

        def X(g, half):
            return lambda: xr_piece(x_raw[g], xq[g], xs[g], half, "S")

        def R(g, half):
            return lambda: xr_piece(r_raw[g], rq[g], rs[g], half, "S")

        def C(g, hb):
            return lambda: c_piece(g, hb, "S")

        def A(i):
            pair, q = divmod(i, NG)

            def run():
                if q == 0:
                    for j in (2 * pair + 4, 2 * pair + 5):
                        if j < N // P:
                            load_a(j)
                a_piece(pair, q, "S")

            return run

        def W(m, gate, eng):
            return lambda: w_piece(m, 1, gate, eng)

        def MIX(j0, h0, w, eng="S"):
            return lambda: mix_piece(j0, h0, w, eng)

        fill = {
            0: [X(1, 0), X(1, 1), R(1, 0), R(1, 1)],
            1: [C(1, 0), C(1, 1)],
            2: [X(2, 0), X(2, 1), R(2, 0), R(2, 1)],
            3: [C(2, 0), C(2, 1), A(0), A(1)],
            4: [A(2), A(3), C(0, 2)],
            5: [A(4), A(5), C(1, 2)],
            6: [A(6), A(7), A(8), C(2, 2)],
            7: [A(9), A(10), A(11), C(0, 3)],
            8: [A(12), A(13), A(14), C(1, 3)],
            9: [A(15), A(16), A(17), C(2, 3)],
            10: [MIX(0, 0, 256), MIX(2, 0, 256), MIX(4, 0, 256)],
            11: [MIX(6, 0, 256), MIX(8, 0, 256), MIX(10, 0, 256)],
        }
        wfill = {
            1: [W("wx", 0, "V"), W("wr", 0, "S")],
            2: [W("wx", 1, "V"), W("wr", 1, "S")],
            3: [W("wx", 2, "V"), W("wr", 2, "S")],
            4: [W("wx", 3, "V"), W("wr", 3, "S")],
        }
        loads = {0: [("wx", 0), ("wr", 0), ("wx", 1), ("wr", 1)], 1: [("wx", 2), ("wr", 2), ("wx", 3), ("wr", 3)]}

        last = len(units) - 1
        for s in range(len(units) + 1):
            if s <= last:
                for m, gate in loads.get(s, []):
                    load_w(m, 1, gate)
                if s == 1:
                    load_a(2)
                    load_a(3)
                hb, g = units[s]
                cc = cT[g, hb]
                ui = work.tile([P, GROUP], F32, name="ui", tag="ui")
                uf = work.tile([P, GROUP], F32, name="uf", tag="uf")
                gg = work.tile([P, GROUP], F32, name="gg", tag="gg")
                nc.vector.scalar_tensor_tensor(out=ui[:], in0=cc[:], scalar=peep_col(0, hb), in1=z[s, 0][:], op0=ALU.mult, op1=ALU.add)
                nc.vector.scalar_tensor_tensor(out=uf[:], in0=cc[:], scalar=peep_col(1, hb), in1=z[s, 1][:], op0=ALU.mult, op1=ALU.add)
                nc.scalar.activation(out=gg[:], in_=z[s, 2][:], func=ACT.Tanh, bias=bias_col(2, hb))
                nc.scalar.activation(out=ui[:], in_=ui[:], func=ACT.Sigmoid, bias=bias_col(0, hb))
                nc.scalar.activation(out=uf[:], in_=uf[:], func=ACT.Sigmoid, bias=bias_col(1, hb))
            if s == 0:
                flush()
            if s <= last:
                z_mm(s, 3)
            else:
                for j0, eng in ((0, "S"), (4, "V"), (8, "S")):
                    mix_piece(j0, 256, 128, eng)
            if s > 0:
                cn_out(s - 1)
                m_mul(s - 1)
            old = list(pending)
            pending.clear()
            for f in fill.get(s, []):
                f()
            new = list(pending)
            pending.clear()
            if s > 0:
                m_transpose(s - 1)
            if s < last:
                for gate in range(3):
                    z_mm(s + 1, gate)
            if s <= last:
                nc.vector.tensor_mul(out=ui[:], in0=ui[:], in1=gg[:])
                for q in old[:2]:
                    q()
                nc.vector.tensor_mul(out=uf[:], in0=uf[:], in1=cc[:])
                for f in wfill.get(s, [])[:1]:
                    f()
            for q in old[2:]:
                q()
            if s <= last:
                cn = work.tile([P, GROUP], F32, name="cn", tag="cn")
                nc.vector.tensor_add(out=cn[:], in0=ui[:], in1=uf[:])
                th = work.tile([P, GROUP], F32, name="th", tag="th")
                nc.scalar.activation(out=th[:], in_=cn[:], func=ACT.Tanh)
            quant = m_evac(s - 1) if s > 0 else None
            if s in (0, 2):
                for q in new:
                    q()
                new = []
            if s <= last:
                uo = work.tile([P, GROUP], F32, name="uo", tag="uo")
                nc.vector.scalar_tensor_tensor(out=uo[:], in0=cn[:], scalar=peep_col(2, hb), in1=z[s, 3][:], op0=ALU.mult, op1=ALU.add)
                nc.scalar.activation(out=uo[:], in_=uo[:], func=ACT.Sigmoid, bias=bias_col(3, hb))
                state[s] = {"o": uo, "th": th, "cn": cn}
            for f in wfill.get(s, [])[1:]:
                f()
            pending.extend(new)
            if quant is not None:
                quant()

        for j0, eng in ((0, "V"), (4, "S"), (8, "V")):
            mix_piece(j0, 384, 128, eng)
